import numpy as np, ml_dtypes
CORES = [10,34,74,98]
N = 4
import mx_ref
BF = ml_dtypes.bfloat16
def f(rng, *shape):
    return mx_ref.flush((rng.standard_normal(shape, dtype=np.float32) * np.exp2(rng.integers(-2, 3, shape[:-1] + (1,)))).astype(BF))
def wide(rng, *shape, cols=0):
    v = rng.standard_normal(shape, dtype=np.float32) * np.exp2(rng.integers(-12, 13, shape)).astype(np.float32)
    if cols: v *= np.repeat(np.exp2(rng.integers(-cols, cols + 1, shape[:-2] + (1, shape[-1] // 4))) * (rng.random(shape[:-2] + (1, shape[-1] // 4)) > 0.0625), 4, axis=-1).astype(np.float32)
    return mx_ref.flush(v.astype(BF))
R, XC = 2048, 512
def lists(rng):
    return rng.integers(0, R, (N, N, 512))
def picks(L):
    return np.ascontiguousarray(L.reshape(N, N, 128, 4).transpose(0, 2, 1, 3)).reshape(N, 128, 4 * N).astype(np.int32)
def setup_inputs(rng):
    return {"x": f(rng, N, R, XC), "w": f(rng, N, R, 128), "pick": picks(lists(rng))}
def setup_inputs_alike(rng):
    d = setup_inputs(rng); L = lists(rng)
    L[:] = L[0, 0].copy()
    d["pick"] = picks(L); return d
def setup_inputs_giant(rng):
    d = setup_inputs(rng); L = lists(rng); big = {}
    for n in ("x", "w"):
        big[n] = 32 * np.arange(R // 32) + rng.integers(0, 32, (N, R // 32))
        m = np.ones((N, R, 1), np.float32)
        for r in range(N): m[r, big[n][r]] = 4096
        d[n] = (d[n].astype(np.float32) * m).astype(BF)
    for r in range(N):
        for s in range(N):
            for g in range(16):
                a, b = 32 * g + rng.permutation(32)[:2]
                L[r, s, a] = rng.choice(big["x"][s]); L[r, s, b] = rng.choice(big["w"][r])
    d["pick"] = picks(L); return d
def setup_inputs_repeat(rng):
    d = setup_inputs(rng); L = lists(rng)
    for r in range(N): L[r, (r + rng.integers(1, N)) % N] = rng.integers(0, R)
    d["pick"] = picks(L); return d
def setup_inputs_sorted(rng):
    d = setup_inputs(rng); L = lists(rng)
    L[:, :, 0] = 0; L[:, :, 1] = R - 1
    d["pick"] = picks(np.sort(L, axis=2)); return d
def setup_inputs_spread(rng):
    d = setup_inputs(rng); d["x"] = wide(rng, N, R, XC); d["w"] = wide(rng, N, R, 128); return d
def check_inputs(d):
    b = []
    for n in ("x", "w"):
        a = np.abs(np.asarray(d[n]).astype(np.float32))
        if not np.isfinite(a).all() or ((a != 0) & ((a < 2.0 ** -30) | (a > 2.0 ** 30))).any(): b.append(n)
    if d["pick"].min() < 0 or d["pick"].max() >= R: b.append("pick")
    return b
def rowtile(v, k):
    return np.ascontiguousarray(v[k].transpose(0, 2, 1)).reshape(128, -1)
def reference(x, w, pick):
    y = np.zeros((N, 128, N * XC), np.float32)
    for r in range(N):
        for s in range(N):
            k = pick[r][:, 4 * s:4 * s + 4]
            y[r][:, XC * s:XC * s + XC] = mx_ref.matmul(mx_ref.quantize(rowtile(w[r], k)), mx_ref.quantize(rowtile(x[s], k)))
    return {"y": y}

@@ -1,0 +1,258 @@
+from concourse.bass import DstId, RemoteDMATransfer, IndirectOffsetOnAxis
+from concourse.mybir import dt, AluOpType, ActivationFunctionType
+
+NR = 4
+XC = 512
+WC = 128
+ROWS = 2048
+
+SCRATCH = {
+    "pk": ("sbuf", [128, 16], "int32"),
+    "plo": ("sbuf", [128, 16], "int32"),
+    "phi": ("sbuf", [128, 16], "int32"),
+    "pls": ("sbuf", [128, 16], "int32"),
+    "pf": ("sbuf", [128, 128], "float32"),
+    "offs": ("sbuf", [128, 128], "uint16"),
+    "ones": ("sbuf", [128, 128], "float32"),
+    "ident": ("sbuf", [128, 128], "float32"),
+    "wb": ("sbuf", [128, 2048], "bfloat16"),
+    "wf": ("sbuf", [128, 2048], "float32"),
+    "wtr": ("sbuf", [128, 2048], "bfloat16"),
+    "wg": ("sbuf", [128, 2048], "float32"),
+    "ys": ("sbuf", [128, 2048], "float32"),
+    "ps_p": ("psum", [128, 512], "float32"),
+    "ps_w": ("psum", [128, 1024], "float32"),
+    "ps_v": ("psum", [128, 1024], "float32"),
+    "ps_y": ("psum", [128, 1536], "float32"),
+}
+for _k in range(NR):
+    SCRATCH["xs%d" % _k] = ("sbuf", [128, 2048], "bfloat16")
+    SCRATCH["xt%d" % _k] = ("sbuf", [128, 2048], "bfloat16")
+    SCRATCH["xq%d" % _k] = ("sbuf", [128, XC], "float8_e4m3fn_x4")
+    SCRATCH["xp%d" % _k] = ("sbuf", [128, XC], "uint8")
+    SCRATCH["wt%d" % _k] = ("sbuf", [128, 512], "bfloat16")
+    SCRATCH["wq%d" % _k] = ("sbuf", [128, WC], "float8_e4m3fn_x4")
+    SCRATCH["wp%d" % _k] = ("sbuf", [128, WC], "uint8")
+    if _k:
+        SCRATCH["li%d" % _k] = ("sbuf", [128, 4], "int32")
+        SCRATCH["rq%d" % _k] = ("sbuf", [128, XC], "float8_e4m3fn_x4")
+        SCRATCH["rp%d" % _k] = ("sbuf", [128, XC], "uint8")
+
+SEMAPHORES = ["id0", "id1", "pk", "wl", "pa", "pb", "pc", "pf", "pt", "off", "wcv", "wcs", "gv", "gs", "lsent", "csent",
+              "mm1", "mm2", "mm0", "mm3a", "mm3b", "ev1", "ev2", "ev0", "ev3a", "ev3b",
+              "st1", "st2", "st0", "st3a", "st3b"]
+SEMAPHORES += ["%s%d" % (n, k) for n in ("wi", "we", "wv", "wd", "qw", "xc", "qx") for k in range(NR)]
+SEMAPHORES += ["%s%d" % (n, k) for n in ("lst", "arr") for k in range(1, NR)]
+SEMAPHORES += ["ga%d%d" % (k, t) for k in range(NR) for t in range(4)]
+
+COPY = ActivationFunctionType.Copy
+
+
+def rank_program(g, core, T, topo):
+    me = T.rank_of(core)
+    if me is None:
+        return
+    S = T.sem
+    cores = T.cores
+    v, a, te, sy = g.vector, g.scalar, g.tensor, g.sync
+
+    def direct(k):
+        return sum(1 for r in range(NR)
+                   if topo.same_plane(topo.chip(cores[r]), topo.chip(cores[(r + k) % NR])))
+    steps = [0] + sorted(range(1, NR), key=direct)
+    to = [(me + steps[k]) % NR for k in range(NR)]
+    frm = [(me - steps[k]) % NR for k in range(NR)]
+
+    def dst(r):
+        rid, pid, _ = topo.addr(cores[r])
+        return rid, pid
+
+    def bits(engs):
+        return sum(1 << e for e in engs)
+
+    sy.dma_start(T.pk[:], T.pick[:]).then_inc(S.pk, 16)
+    sy.dma_start(T.wb[:], T.w[:]).then_inc(S.wl, 16)
+
+    v.memset(T.ones[:], 1.0).then_inc(S.id0, 1)
+    v.wait_ge(S.pk, 16)
+    v.tensor_scalar(T.plo[:], T.pk[:], 15, None, AluOpType.bitwise_and).then_inc(S.pa, 1)
+    v.tensor_scalar(T.phi[:], T.pk[:], 4, None, AluOpType.arith_shift_right).then_inc(S.pb, 1)
+    v.wait_ge(S.pa, 1)
+    v.tensor_scalar(T.pls[:], T.plo[:], 128, None, AluOpType.mult).then_inc(S.pc, 1)
+    v.wait_ge(S.pb, 1)
+    v.wait_ge(S.pc, 1)
+    for q in range(8):
+        v.tensor_tensor(T.pf[:, 16 * q:16 * q + 16], T.pls[:], T.phi[:], AluOpType.add).then_inc(S.pf, 1)
+    v.wait_ge(S.pt, 1)
+    v.tensor_copy(T.offs[:], T.ps_p[:, 0:128]).then_inc(S.off, 1)
+    v.wait_ge(S.wl, 16)
+    v.tensor_copy(T.wf[:, 0:1024], T.wb[:, 0:1024]).then_inc(S.wcv, 1)
+    for b in (1, 3):
+        v.wait_ge(S["wi%d" % b], 4)
+        v.tensor_copy(T.wtr[:, 512 * b:512 * b + 512], T.ps_w[:, 512:1024]).then_inc(S["we%d" % b], 1)
+    v.wait_ge(S.off, 1)
+    for b in range(4):
+        v.wait_ge(S["we%d" % b], 1)
+    v.tensor_copy(T.wg[:, 0:1024], T.wtr[:].indirect(T.offs[:, 0:64])).then_inc(S.gv, 1)
+
+    a.wait_ge(S.wl, 16)
+    a.activation(T.wf[:, 1024:2048], T.wb[:, 1024:2048], COPY).then_inc(S.wcs, 1)
+    for b in (0, 2):
+        a.wait_ge(S["wi%d" % b], 4)
+        a.activation(T.wtr[:, 512 * b:512 * b + 512], T.ps_w[:, 0:512], COPY).then_inc(S["we%d" % b], 1)
+    a.wait_ge(S.off, 1)
+    for b in range(4):
+        a.wait_ge(S["we%d" % b], 1)
+    a.activation(T.wg[:, 1024:2048], T.wtr[:].indirect(T.offs[:, 64:128]), COPY).then_inc(S.gs, 1)
+
+    te.wait_ge(S.id1, 1)
+    te.wait_ge(S.pf, 8)
+    te.transpose(T.ps_p[:, 0:128], T.pf[:], T.ident[:]).then_inc(S.pt, 1)
+    for b in range(4):
+        if b == 0:
+            te.wait_ge(S.wcv, 1)
+        if b == 2:
+            te.wait_ge(S.wcs, 1)
+        if b >= 2:
+            te.wait_ge(S["we%d" % (b - 2)], 1)
+        for i in range(4):
+            c = 4 * b + i
+            o = 512 * (b % 2) + 128 * i
+            te.transpose(T.ps_w[:, o:o + 128], T.wf[:, 128 * c:128 * c + 128], T.ident[:]).then_inc(S["wi%d" % b], 1)
+    worder = [1, 2, 0, 3]
+    te.wait_ge(S.gv, 1)
+    te.wait_ge(S.gs, 1)
+    for n, k in enumerate(worder):
+        if n >= 2:
+            te.wait_ge(S["wd%d" % worder[n - 2]], 4)
+        s = frm[k]
+        for t in range(4):
+            o = 512 * (n % 2) + 128 * t
+            c = 4 * s + t
+            te.transpose(T.ps_v[:, o:o + 128], T.wg[:, c:2048:16], T.ident[:]).then_inc(S["wv%d" % k], 1)
+
+    for n, k in enumerate(worder):
+        a.wait_ge(S["wv%d" % k], 4)
+        for t in range(4):
+            o = 512 * (n % 2) + 128 * t
+            a.activation(T["wt%d" % k][:, t:512:4], T.ps_v[:, o:o + 128], COPY).then_inc(S["wd%d" % k], 1)
+
+    def xtile(k):
+        for t in range(4):
+            v.wait_ge(S["ga%d%d" % (k, t)], 16)
+            v.tensor_copy(T["xt%d" % k][:, t:2048:4], T["xs%d" % k][:, 512 * t:512 * t + 512]).then_inc(S["xc%d" % k], 1)
+        v.wait_ge(S["xc%d" % k], 4)
+        v.quantize_mx(T["xq%d" % k][:], T["xp%d" % k][:], T["xt%d" % k][:]).then_inc(S["qx%d" % k], 1)
+
+    xtile(1)
+    xtile(2)
+    for k in worder:
+        v.wait_ge(S["wd%d" % k], 4)
+        v.quantize_mx(T["wq%d" % k][:], T["wp%d" % k][:], T["wt%d" % k][:]).then_inc(S["qw%d" % k], 1)
+    xtile(3)
+    xtile(0)
+
+    g.wait_ge(S.id0, 1)
+    g.affine_select(T.ident[:], T.ones[:], [[-1, 128]], AluOpType.is_equal, 0.0, 0, 1).then_inc(S.id1, 1)
+
+    def listmove(k, engs):
+        s = frm[k]
+        rid, pid = dst(s)
+        return RemoteDMATransfer(dst_ids=[DstId(rid=rid, pnc=pid)], dma_engine_mask=bits(engs),
+                                 remote_sem=S["lst%d" % k],
+                                 srcs=[T.pk[:, 4 * s:4 * s + 4]], dsts=[T["li%d" % k][:]])
+
+    def gather(k, t):
+        idx = T["li%d" % k][:, t:t + 1] if k else T.pk[:, 4 * me + t:4 * me + t + 1]
+        g.indirect_dma_start(T["xs%d" % k][:, 512 * t:512 * t + 512], None, T.x[:],
+                             IndirectOffsetOnAxis(ap=idx, axis=0), bounds_check=ROWS - 1).then_inc(S["ga%d%d" % (k, t)], 16)
+
+    def send_fused(k):
+        e = topo.engines(core, cores[to[k]])
+        rid, pid = dst(to[k])
+        parts = [e[0:2], e[2:4], e[4:6], e[6:7], e[7:8]]
+        tr = []
+        for i, p in enumerate(parts):
+            if i < 4:
+                src = T["xq%d" % k][:, 128 * i:128 * i + 128].bitcast(dt.uint8)
+                d = T["rq%d" % k][:, 128 * i:128 * i + 128].bitcast(dt.uint8)
+            else:
+                src, d = T["xp%d" % k][:], T["rp%d" % k][:]
+            tr.append(RemoteDMATransfer(dst_ids=[DstId(rid=rid, pnc=pid)], dma_engine_mask=bits(p),
+                                        remote_sem=S["arr%d" % k], srcs=[src], dsts=[d]))
+        g.remote_dma_fused(tr, local_sem=S.csent)
+        return sum(len(p) for p in parts)
+
+    def send_two(k):
+        e = topo.engines(core, cores[to[k]])
+        rid, pid = dst(to[k])
+        g.remote_dma(T["rq%d" % k][:].bitcast(dt.uint8), T["xq%d" % k][:].bitcast(dt.uint8),
+                     S["arr%d" % k], S.csent, pid, rid, bits(e))
+        g.remote_dma(T["rp%d" % k][:], T["xp%d" % k][:], S["arr%d" % k], S.csent, pid, rid, bits(e))
+        return 2 * len(e)
+
+    off_chip = topo.engines(core, cores[frm[1]])
+    la, lb, lc = off_chip[0:4], off_chip[4:6], off_chip[6:8]
+    g.wait_ge(S.pk, 16)
+    g.remote_dma_fused([listmove(1, la)], local_sem=S.lsent)
+    gather(0, 0)
+    g.remote_dma_fused([listmove(2, lb), listmove(3, lc)], local_sem=S.lsent)
+    gather(0, 1)
+    g.wait_ge(S.lst1, len(la))
+    for t in range(4):
+        gather(1, t)
+    g.wait_ge(S.lst2, len(lb))
+    for t in range(3):
+        gather(2, t)
+    g.wait_ge(S.qx1, 1)
+    n1 = send_fused(1)
+    gather(2, 3)
+    g.wait_ge(S.lst3, len(lc))
+    for t in range(3):
+        gather(3, t)
+    g.wait_ge(S.qx2, 1)
+    n2 = send_fused(2)
+    gather(3, 3)
+    gather(0, 2)
+    gather(0, 3)
+    g.wait_ge(S.qx3, 1)
+    n3 = send_two(3)
+    g.wait_ge(S.lsent, len(la) + len(lb) + len(lc))
+    g.wait_ge(S.csent, n1 + n2 + n3)
+
+    te.wait_ge(S.qw1, 1)
+    te.wait_ge(S.arr1, n1)
+    te.matmul_mx(T.ps_y[:, 0:512], T.wq1[:], T.wp1[:], T.rq1[:], T.rp1[:], True, True).then_inc(S.mm1, 1)
+    te.wait_ge(S.qw2, 1)
+    te.wait_ge(S.arr2, n2)
+    te.matmul_mx(T.ps_y[:, 512:1024], T.wq2[:], T.wp2[:], T.rq2[:], T.rp2[:], True, True).then_inc(S.mm2, 1)
+    te.wait_ge(S.qw0, 1)
+    te.wait_ge(S.qx0, 1)
+    te.matmul_mx(T.ps_y[:, 1024:1536], T.wq0[:], T.wp0[:], T.xq0[:], T.xp0[:], True, True).then_inc(S.mm0, 1)
+    te.wait_ge(S.qw3, 1)
+    te.wait_ge(S.ev1, 1)
+    te.wait_ge(S.ev2, 1)
+    te.wait_ge(S.arr3, n3)
+    te.matmul_mx(T.ps_y[:, 0:256], T.wq3[:], T.wp3[:], T.rq3[:, 0:256], T.rp3[:, 0:256], True, True).then_inc(S.mm3a, 1)
+    te.matmul_mx(T.ps_y[:, 512:768], T.wq3[:], T.wp3[:], T.rq3[:, 256:512], T.rp3[:, 256:512], True, True).then_inc(S.mm3b, 1)
+
+    def ycols(k, lo=0, hi=XC):
+        b = XC * frm[k]
+        return slice(b + lo, b + hi)
+
+    for k, o in ((1, 0), (2, 512), (0, 1024)):
+        a.wait_ge(S["mm%d" % k], 1)
+        a.activation(T.ys[:, ycols(k)], T.ps_y[:, o:o + 512], COPY).then_inc(S["ev%d" % k], 1)
+        sy.wait_ge(S["ev%d" % k], 1)
+        sy.dma_start(T.y[:, ycols(k)], T.ys[:, ycols(k)]).then_inc(S["st%d" % k], 16)
+    v.wait_ge(S.mm3a, 1)
+    v.tensor_copy(T.ys[:, ycols(3, 0, 256)], T.ps_y[:, 0:256]).then_inc(S.ev3a, 1)
+    sy.wait_ge(S.ev3a, 1)
+    sy.dma_start(T.y[:, ycols(3, 0, 256)], T.ys[:, ycols(3, 0, 256)]).then_inc(S.st3a, 16)
+    a.wait_ge(S.mm3b, 1)
+    a.activation(T.ys[:, ycols(3, 256, 512)], T.ps_y[:, 512:768], COPY).then_inc(S.ev3b, 1)
+    a.wait_ge(S.ev3b, 1)
+    a.dma_start(T.y[:, ycols(3, 256, 512)], T.ys[:, ycols(3, 256, 512)]).then_inc(S.st3b, 16)
+    for n in ("st1", "st2", "st0", "st3a"):
+        sy.wait_ge(S[n], 16)
+    a.wait_ge(S.st3b, 16)

@@ -5,6 +5,7 @@ NR = 4
 XC = 512
 WC = 128
 ROWS = 2048
+WIN = 3
 
 SCRATCH = {
     "pk": ("sbuf", [128, 16], "int32"),
@@ -13,21 +14,34 @@ SCRATCH = {
     "pls": ("sbuf", [128, 16], "int32"),
     "pf": ("sbuf", [128, 128], "float32"),
     "offs": ("sbuf", [128, 128], "uint16"),
+    "lu": ("sbuf", [128, 4], "int32"),
+    "lb": ("sbuf", [128, 4], "int32"),
+    "lc": ("sbuf", [128, 4], "int32"),
+    "lv": ("sbuf", [128, 4], "int32"),
+    "lw": ("sbuf", [128, 4], "int32"),
+    "lp": ("sbuf", [128, 4], "int32"),
+    "pf3": ("sbuf", [128, 128], "float32"),
+    "offs3": ("sbuf", [128, 128], "uint16"),
     "ones": ("sbuf", [128, 128], "float32"),
     "ident": ("sbuf", [128, 128], "float32"),
     "wb": ("sbuf", [128, 2048], "bfloat16"),
     "wf": ("sbuf", [128, 2048], "float32"),
     "wtr": ("sbuf", [128, 2048], "bfloat16"),
     "wg": ("sbuf", [128, 2048], "float32"),
+    "xb": ("sbuf", [128, 8192], "bfloat16"),
+    "xv": ("sbuf", [128, 8192], "bfloat16"),
+    "xg": ("sbuf", [128, 2048], "float32"),
+    "x3": ("sbuf", [128, 4, 512], "bfloat16"),
     "ys": ("sbuf", [128, 2048], "float32"),
     "ps_p": ("psum", [128, 512], "float32"),
     "ps_w": ("psum", [128, 1024], "float32"),
-    "ps_v": ("psum", [128, 1024], "float32"),
+    "ps_x": ("psum", [128, 1024], "float32"),
     "ps_y": ("psum", [128, 1536], "float32"),
 }
 for _k in range(NR):
-    SCRATCH["xs%d" % _k] = ("sbuf", [128, 2048], "bfloat16")
-    SCRATCH["xt%d" % _k] = ("sbuf", [128, 2048], "bfloat16")
+    if _k != WIN:
+        SCRATCH["xs%d" % _k] = ("sbuf", [128, 2048], "bfloat16")
+        SCRATCH["xt%d" % _k] = ("sbuf", [128, 2048], "bfloat16")
     SCRATCH["xq%d" % _k] = ("sbuf", [128, XC], "float8_e4m3fn_x4")
     SCRATCH["xp%d" % _k] = ("sbuf", [128, XC], "uint8")
     SCRATCH["wt%d" % _k] = ("sbuf", [128, 512], "bfloat16")
@@ -38,14 +52,17 @@ for _k in range(NR):
         SCRATCH["rq%d" % _k] = ("sbuf", [128, XC], "float8_e4m3fn_x4")
         SCRATCH["rp%d" % _k] = ("sbuf", [128, XC], "uint8")
 
-SEMAPHORES = ["id0", "id1", "pk", "wl", "pa", "pb", "pc", "pf", "pt", "off", "wcv", "wcs", "gv", "gs", "lsent", "csent",
+SEMAPHORES = ["id0", "id1", "pk", "wl", "pa", "pb", "pc", "pf", "pt", "off", "wc0", "wc1", "gs",
+              "ls1", "lsent", "csent", "la", "lv", "lw", "lp", "lm", "ld1", "ld2", "ld3", "pt3", "off3",
+              "xz", "hv", "hs",
               "mm1", "mm2", "mm0", "mm3a", "mm3b", "ev1", "ev2", "ev0", "ev3a", "ev3b",
               "st1", "st2", "st0", "st3a", "st3b"]
-SEMAPHORES += ["%s%d" % (n, k) for n in ("wi", "we", "wv", "wd", "qw", "xc", "qx") for k in range(NR)]
+SEMAPHORES += ["%s%d" % (n, k) for n in ("wi", "we", "wv", "wd", "qw", "xc", "qx", "xl", "xf", "xe") for k in range(NR)]
 SEMAPHORES += ["%s%d" % (n, k) for n in ("lst", "arr") for k in range(1, NR)]
-SEMAPHORES += ["ga%d%d" % (k, t) for k in range(NR) for t in range(4)]
+SEMAPHORES += ["ga%d%d" % (k, t) for k in range(NR) if k != WIN for t in range(4)]
 
 COPY = ActivationFunctionType.Copy
+AND, SHR, ADD, MULT = AluOpType.bitwise_and, AluOpType.arith_shift_right, AluOpType.add, AluOpType.mult
 
 
 def rank_program(g, core, T, topo):
@@ -62,6 +79,7 @@ def rank_program(g, core, T, topo):
     steps = [0] + sorted(range(1, NR), key=direct)
     to = [(me + steps[k]) % NR for k in range(NR)]
     frm = [(me - steps[k]) % NR for k in range(NR)]
+    worder = [1, 0, 2, 3]
 
     def dst(r):
         rid, pid, _ = topo.addr(cores[r])
@@ -70,87 +88,165 @@ def rank_program(g, core, T, topo):
     def bits(engs):
         return sum(1 << e for e in engs)
 
+    off_chip = topo.engines(core, cores[frm[1]])
+    la, lb, lc = off_chip[0:4], off_chip[4:6], off_chip[6:8]
+
     sy.dma_start(T.pk[:], T.pick[:]).then_inc(S.pk, 16)
     sy.dma_start(T.wb[:], T.w[:]).then_inc(S.wl, 16)
+    for n in range(16):
+        z, q = n // 4, n % 4
+        if n == 2:
+            sy.wait_ge(S.ls1, len(la))
+        if q == 0 and z >= 2:
+            sy.wait_ge(S["xl%d" % (z - 2)], 64)
+        sy.dma_start(T.xb[32 * q:32 * q + 32, 2048 * z:2048 * z + 2048],
+                     T.x[512 * z:512 * z + 512, 128 * q:128 * q + 128]).then_inc(S["xl%d" % z], 16)
 
     v.memset(T.ones[:], 1.0).then_inc(S.id0, 1)
     v.wait_ge(S.pk, 16)
-    v.tensor_scalar(T.plo[:], T.pk[:], 15, None, AluOpType.bitwise_and).then_inc(S.pa, 1)
-    v.tensor_scalar(T.phi[:], T.pk[:], 4, None, AluOpType.arith_shift_right).then_inc(S.pb, 1)
+    v.tensor_scalar(T.plo[:], T.pk[:], 15, None, AND).then_inc(S.pa, 1)
+    v.tensor_scalar(T.phi[:], T.pk[:], 4, None, SHR).then_inc(S.pb, 1)
     v.wait_ge(S.pa, 1)
-    v.tensor_scalar(T.pls[:], T.plo[:], 128, None, AluOpType.mult).then_inc(S.pc, 1)
+    v.tensor_scalar(T.pls[:], T.plo[:], 128, None, MULT).then_inc(S.pc, 1)
     v.wait_ge(S.pb, 1)
     v.wait_ge(S.pc, 1)
     for q in range(8):
-        v.tensor_tensor(T.pf[:, 16 * q:16 * q + 16], T.pls[:], T.phi[:], AluOpType.add).then_inc(S.pf, 1)
+        v.tensor_tensor(T.pf[:, 16 * q:16 * q + 16], T.pls[:], T.phi[:], ADD).then_inc(S.pf, 1)
+    v.wait_ge(S.wl, 16)
+    for h in range(2):
+        v.tensor_copy(T.wf[:, 1024 * h:1024 * h + 1024], T.wb[:, 1024 * h:1024 * h + 1024]).then_inc(S["wc%d" % h], 1)
     v.wait_ge(S.pt, 1)
     v.tensor_copy(T.offs[:], T.ps_p[:, 0:128]).then_inc(S.off, 1)
-    v.wait_ge(S.wl, 16)
-    v.tensor_copy(T.wf[:, 0:1024], T.wb[:, 0:1024]).then_inc(S.wcv, 1)
-    for b in (1, 3):
-        v.wait_ge(S["wi%d" % b], 4)
-        v.tensor_copy(T.wtr[:, 512 * b:512 * b + 512], T.ps_w[:, 512:1024]).then_inc(S["we%d" % b], 1)
-    v.wait_ge(S.off, 1)
-    for b in range(4):
-        v.wait_ge(S["we%d" % b], 1)
-    v.tensor_copy(T.wg[:, 0:1024], T.wtr[:].indirect(T.offs[:, 0:64])).then_inc(S.gv, 1)
+    li = T["li%d" % WIN]
+    v.wait_ge(S["lst%d" % WIN], len(lc))
+    v.tensor_scalar(T.lu[:], li[:], 5, 48, SHR, AND).then_inc(S.la, 1)
+    v.tensor_scalar(T.lb[:], li[:], 15, None, AND).then_inc(S.la, 1)
+    v.tensor_scalar(T.lc[:], li[:], 4, 31, SHR, AND).then_inc(S.la, 1)
+    v.wait_ge(S.la, 3)
+    v.tensor_tensor(T.lv[:], T.lu[:], T.lb[:], ADD).then_inc(S.lv, 1)
+    v.wait_ge(S.lv, 1)
+    v.tensor_scalar(T.lw[:], T.lv[:], 128, None, MULT).then_inc(S.lw, 1)
+    v.wait_ge(S.lw, 1)
+    v.tensor_tensor(T.lp[:], T.lw[:], T.lc[:], ADD).then_inc(S.lp, 1)
+    v.wait_ge(S.lp, 1)
+    for m in range(4):
+        v.tensor_scalar(T.pf3[:, 4 * m:4 * m + 4], T.lp[:], 32 * m, None, ADD).then_inc(S.lm, 1)
+    v.wait_ge(S.lm, 4)
+    v.tensor_copy(T.pf3[:, 16:32], T.pf3[:, 0:16]).then_inc(S.ld1, 1)
+    v.wait_ge(S.ld1, 1)
+    v.tensor_copy(T.pf3[:, 32:64], T.pf3[:, 0:32]).then_inc(S.ld2, 1)
+    v.wait_ge(S.ld2, 1)
+    v.tensor_copy(T.pf3[:, 64:128], T.pf3[:, 0:64]).then_inc(S.ld3, 1)
 
-    a.wait_ge(S.wl, 16)
-    a.activation(T.wf[:, 1024:2048], T.wb[:, 1024:2048], COPY).then_inc(S.wcs, 1)
-    for b in (0, 2):
+    for b in range(4):
         a.wait_ge(S["wi%d" % b], 4)
-        a.activation(T.wtr[:, 512 * b:512 * b + 512], T.ps_w[:, 0:512], COPY).then_inc(S["we%d" % b], 1)
+        o = 512 * (b % 2)
+        a.activation(T.wtr[:, 512 * b:512 * b + 512], T.ps_w[:, o:o + 512], COPY).then_inc(S["we%d" % b], 1)
     a.wait_ge(S.off, 1)
     for b in range(4):
         a.wait_ge(S["we%d" % b], 1)
-    a.activation(T.wg[:, 1024:2048], T.wtr[:].indirect(T.offs[:, 64:128]), COPY).then_inc(S.gs, 1)
+    a.activation(T.wg[:], T.wtr[:].indirect(T.offs[:, 0:128]), COPY).then_inc(S.gs, 1)
 
     te.wait_ge(S.id1, 1)
     te.wait_ge(S.pf, 8)
     te.transpose(T.ps_p[:, 0:128], T.pf[:], T.ident[:]).then_inc(S.pt, 1)
     for b in range(4):
-        if b == 0:
-            te.wait_ge(S.wcv, 1)
-        if b == 2:
-            te.wait_ge(S.wcs, 1)
+        if b % 2 == 0:
+            te.wait_ge(S["wc%d" % (b // 2)], 1)
         if b >= 2:
             te.wait_ge(S["we%d" % (b - 2)], 1)
         for i in range(4):
             c = 4 * b + i
             o = 512 * (b % 2) + 128 * i
             te.transpose(T.ps_w[:, o:o + 128], T.wf[:, 128 * c:128 * c + 128], T.ident[:]).then_inc(S["wi%d" % b], 1)
-    worder = [1, 2, 0, 3]
-    te.wait_ge(S.gv, 1)
-    te.wait_ge(S.gs, 1)
-    for n, k in enumerate(worder):
+    te.wait_ge(S.off, 1)
+    te.wait_ge(S.ld3, 1)
+    te.transpose(T.ps_p[:, 128:256], T.pf3[:], T.ident[:]).then_inc(S.pt3, 1)
+
+    def wturn(n):
+        k, o = worder[n], 512 * (n % 2)
         if n >= 2:
-            te.wait_ge(S["wd%d" % worder[n - 2]], 4)
-        s = frm[k]
+            te.wait_ge(S["wd%d" % worder[n - 2]], 1)
         for t in range(4):
-            o = 512 * (n % 2) + 128 * t
-            c = 4 * s + t
-            te.transpose(T.ps_v[:, o:o + 128], T.wg[:, c:2048:16], T.ident[:]).then_inc(S["wv%d" % k], 1)
+            te.transpose(T.ps_w[:, o + t:o + 512:4], T.wg[:, 4 * frm[k] + t:2048:16], T.ident[:]).then_inc(S["wv%d" % k], 1)
 
-    for n, k in enumerate(worder):
+    def wevac(n):
+        k, o = worder[n], 512 * (n % 2)
         a.wait_ge(S["wv%d" % k], 4)
-        for t in range(4):
-            o = 512 * (n % 2) + 128 * t
-            a.activation(T["wt%d" % k][:, t:512:4], T.ps_v[:, o:o + 128], COPY).then_inc(S["wd%d" % k], 1)
+        a.activation(T["wt%d" % k][:], T.ps_w[:, o:o + 512], COPY).then_inc(S["wd%d" % k], 1)
 
-    def xtile(k):
+    te.wait_ge(S.gs, 1)
+    wturn(0)
+    wturn(1)
+    te.wait_ge(S.hv, 1)
+    te.wait_ge(S.hs, 1)
+    for m in range(4):
+        if m >= 2:
+            te.wait_ge(S["xe%d" % (m - 2)], 1)
+        o = 512 * (m % 2)
         for t in range(4):
-            v.wait_ge(S["ga%d%d" % (k, t)], 16)
-            v.tensor_copy(T["xt%d" % k][:, t:2048:4], T["xs%d" % k][:, 512 * t:512 * t + 512]).then_inc(S["xc%d" % k], 1)
+            te.transpose(T.ps_x[:, o + t:o + 512:4], T.xg[:, 4 * m + t:2048:16], T.ident[:]).then_inc(S["xf%d" % m], 1)
+    wturn(2)
+    wturn(3)
+
+    a.wait_ge(S.off3, 1)
+    a.wait_ge(S.xz, 4)
+    a.activation(T.xg[:, 1024:2048], T.xv[:].indirect(T.offs3[:, 64:128]), COPY).then_inc(S.hs, 1)
+    wevac(0)
+    wevac(1)
+    for m in range(4):
+        a.wait_ge(S["xf%d" % m], 4)
+        o = 512 * (m % 2)
+        a.activation(T.x3[:, :, 128 * m:128 * m + 128], T.ps_x[:, o:o + 512], COPY).then_inc(S["xe%d" % m], 1)
+    wevac(2)
+    wevac(3)
+
+    def xcopy(k, t):
+        v.wait_ge(S["ga%d%d" % (k, t)], 16)
+        v.tensor_copy(T["xt%d" % k][:, t:2048:4], T["xs%d" % k][:, 512 * t:512 * t + 512]).then_inc(S["xc%d" % k], 1)
+
+    def xquant(k):
         v.wait_ge(S["xc%d" % k], 4)
         v.quantize_mx(T["xq%d" % k][:], T["xp%d" % k][:], T["xt%d" % k][:]).then_inc(S["qx%d" % k], 1)
 
-    xtile(1)
-    xtile(2)
-    for k in worder:
-        v.wait_ge(S["wd%d" % k], 4)
+    def wquant(n):
+        k = worder[n]
+        v.wait_ge(S["wd%d" % k], 1)
         v.quantize_mx(T["wq%d" % k][:], T["wp%d" % k][:], T["wt%d" % k][:]).then_inc(S["qw%d" % k], 1)
-    xtile(3)
-    xtile(0)
+
+    def xturn(z):
+        v.wait_ge(S["xl%d" % z], 64)
+        v.transpose(T.xv[:, 2048 * z:2048 * z + 2048], T.xb[:, 2048 * z:2048 * z + 2048]).then_inc(S.xz, 1)
+
+    xturn(0)
+    v.wait_ge(S.pt3, 1)
+    v.tensor_copy(T.offs3[:], T.ps_p[:, 128:256]).then_inc(S.off3, 1)
+    xturn(1)
+    xcopy(1, 0)
+    xcopy(1, 1)
+    xcopy(1, 2)
+    xturn(2)
+    xcopy(1, 3)
+    xquant(1)
+    xturn(3)
+    v.wait_ge(S.off3, 1)
+    v.wait_ge(S.xz, 4)
+    v.tensor_copy(T.xg[:, 0:1024], T.xv[:].indirect(T.offs3[:, 0:64])).then_inc(S.hv, 1)
+    for t in range(4):
+        xcopy(2, t)
+    xquant(2)
+    for m in range(4):
+        v.wait_ge(S["xe%d" % m], 1)
+    for q in range(4):
+        v.quantize_mx(T["xq%d" % WIN][:, 128 * q:128 * q + 128], T["xp%d" % WIN][:, 128 * q:128 * q + 128],
+                      T.x3[:, q, :]).then_inc(S["qx%d" % WIN], 1)
+    wquant(0)
+    wquant(1)
+    for t in range(4):
+        xcopy(0, t)
+    xquant(0)
+    wquant(2)
+    wquant(3)
 
     g.wait_ge(S.id0, 1)
     g.affine_select(T.ident[:], T.ones[:], [[-1, 128]], AluOpType.is_equal, 0.0, 0, 1).then_inc(S.id1, 1)
@@ -191,10 +287,8 @@ def rank_program(g, core, T, topo):
         g.remote_dma(T["rp%d" % k][:], T["xp%d" % k][:], S["arr%d" % k], S.csent, pid, rid, bits(e))
         return 2 * len(e)
 
-    off_chip = topo.engines(core, cores[frm[1]])
-    la, lb, lc = off_chip[0:4], off_chip[4:6], off_chip[6:8]
     g.wait_ge(S.pk, 16)
-    g.remote_dma_fused([listmove(1, la)], local_sem=S.lsent)
+    g.remote_dma_fused([listmove(1, la)], local_sem=S.ls1)
     gather(0, 0)
     g.remote_dma_fused([listmove(2, lb), listmove(3, lc)], local_sem=S.lsent)
     gather(0, 1)
@@ -207,31 +301,30 @@ def rank_program(g, core, T, topo):
     g.wait_ge(S.qx1, 1)
     n1 = send_fused(1)
     gather(2, 3)
-    g.wait_ge(S.lst3, len(lc))
-    for t in range(3):
-        gather(3, t)
-    g.wait_ge(S.qx2, 1)
-    n2 = send_fused(2)
-    gather(3, 3)
     gather(0, 2)
     gather(0, 3)
-    g.wait_ge(S.qx3, 1)
-    n3 = send_two(3)
-    g.wait_ge(S.lsent, len(la) + len(lb) + len(lc))
+    g.wait_ge(S.qx2, 1)
+    n2 = send_two(2)
+    g.wait_ge(S["qx%d" % WIN], 4)
+    n3 = send_two(WIN)
+    g.wait_ge(S.lsent, len(lb) + len(lc))
     g.wait_ge(S.csent, n1 + n2 + n3)
 
-    te.wait_ge(S.qw1, 1)
-    te.wait_ge(S.arr1, n1)
-    te.matmul_mx(T.ps_y[:, 0:512], T.wq1[:], T.wp1[:], T.rq1[:], T.rp1[:], True, True).then_inc(S.mm1, 1)
-    te.wait_ge(S.qw2, 1)
-    te.wait_ge(S.arr2, n2)
-    te.matmul_mx(T.ps_y[:, 512:1024], T.wq2[:], T.wp2[:], T.rq2[:], T.rp2[:], True, True).then_inc(S.mm2, 1)
-    te.wait_ge(S.qw0, 1)
-    te.wait_ge(S.qx0, 1)
-    te.matmul_mx(T.ps_y[:, 1024:1536], T.wq0[:], T.wp0[:], T.xq0[:], T.xp0[:], True, True).then_inc(S.mm0, 1)
+    bank = {1: 0, 0: 512, 2: 1024}
+    narr = {1: n1, 2: n2}
+    for k in worder[:3]:
+        o = bank[k]
+        te.wait_ge(S["qw%d" % k], 1)
+        if k:
+            te.wait_ge(S["arr%d" % k], narr[k])
+            xq, xp = T["rq%d" % k], T["rp%d" % k]
+        else:
+            te.wait_ge(S.qx0, 1)
+            xq, xp = T.xq0, T.xp0
+        te.matmul_mx(T.ps_y[:, o:o + 512], T["wq%d" % k][:], T["wp%d" % k][:], xq[:], xp[:], True, True).then_inc(S["mm%d" % k], 1)
     te.wait_ge(S.qw3, 1)
     te.wait_ge(S.ev1, 1)
-    te.wait_ge(S.ev2, 1)
+    te.wait_ge(S.ev0, 1)
     te.wait_ge(S.arr3, n3)
     te.matmul_mx(T.ps_y[:, 0:256], T.wq3[:], T.wp3[:], T.rq3[:, 0:256], T.rp3[:, 0:256], True, True).then_inc(S.mm3a, 1)
     te.matmul_mx(T.ps_y[:, 512:768], T.wq3[:], T.wp3[:], T.rq3[:, 256:512], T.rp3[:, 256:512], True, True).then_inc(S.mm3b, 1)
@@ -240,7 +333,8 @@ def rank_program(g, core, T, topo):
         b = XC * frm[k]
         return slice(b + lo, b + hi)
 
-    for k, o in ((1, 0), (2, 512), (0, 1024)):
+    for k in worder[:3]:
+        o = bank[k]
         a.wait_ge(S["mm%d" % k], 1)
         a.activation(T.ys[:, ycols(k)], T.ps_y[:, o:o + 512], COPY).then_inc(S["ev%d" % k], 1)
         sy.wait_ge(S["ev%d" % k], 1)

from concourse.bass import DstId, RemoteDMATransfer, IndirectOffsetOnAxis
from concourse.mybir import dt, AluOpType, ActivationFunctionType

NR = 4
XC = 512
WC = 128
ROWS = 2048
WIN = 3

SCRATCH = {
    "pk": ("sbuf", [128, 16], "int32"),
    "plo": ("sbuf", [128, 16], "int32"),
    "phi": ("sbuf", [128, 16], "int32"),
    "pls": ("sbuf", [128, 16], "int32"),
    "pf": ("sbuf", [128, 128], "float32"),
    "offs": ("sbuf", [128, 128], "uint16"),
    "lu": ("sbuf", [128, 4], "int32"),
    "lb": ("sbuf", [128, 4], "int32"),
    "lc": ("sbuf", [128, 4], "int32"),
    "lv": ("sbuf", [128, 4], "int32"),
    "lw": ("sbuf", [128, 4], "int32"),
    "lp": ("sbuf", [128, 4], "int32"),
    "pf3": ("sbuf", [128, 128], "float32"),
    "offs3": ("sbuf", [128, 128], "uint16"),
    "ones": ("sbuf", [128, 128], "float32"),
    "ident": ("sbuf", [128, 128], "float32"),
    "wb": ("sbuf", [128, 2048], "bfloat16"),
    "wf": ("sbuf", [128, 2048], "float32"),
    "wtr": ("sbuf", [128, 2048], "bfloat16"),
    "wg": ("sbuf", [128, 2048], "float32"),
    "xb": ("sbuf", [128, 8192], "bfloat16"),
    "xv": ("sbuf", [128, 8192], "bfloat16"),
    "xg": ("sbuf", [128, 2048], "float32"),
    "x3": ("sbuf", [128, 4, 512], "bfloat16"),
    "ys": ("sbuf", [128, 2048], "float32"),
    "ps_p": ("psum", [128, 512], "float32"),
    "ps_w": ("psum", [128, 1024], "float32"),
    "ps_x": ("psum", [128, 1024], "float32"),
    "ps_y": ("psum", [128, 1536], "float32"),
}
for _k in range(NR):
    if _k != WIN:
        SCRATCH["xs%d" % _k] = ("sbuf", [128, 2048], "bfloat16")
        SCRATCH["xt%d" % _k] = ("sbuf", [128, 2048], "bfloat16")
    SCRATCH["xq%d" % _k] = ("sbuf", [128, XC], "float8_e4m3fn_x4")
    SCRATCH["xp%d" % _k] = ("sbuf", [128, XC], "uint8")
    SCRATCH["wt%d" % _k] = ("sbuf", [128, 512], "bfloat16")
    SCRATCH["wq%d" % _k] = ("sbuf", [128, WC], "float8_e4m3fn_x4")
    SCRATCH["wp%d" % _k] = ("sbuf", [128, WC], "uint8")
    if _k:
        SCRATCH["li%d" % _k] = ("sbuf", [128, 4], "int32")
        SCRATCH["rq%d" % _k] = ("sbuf", [128, XC], "float8_e4m3fn_x4")
        SCRATCH["rp%d" % _k] = ("sbuf", [128, XC], "uint8")

SEMAPHORES = ["id0", "id1", "pk", "wl", "pa", "pb", "pc", "pf", "pt", "off", "wc0", "wc1", "gs",
              "ls1", "lsent", "csent", "la", "lv", "lw", "lp", "lm", "ld1", "ld2", "ld3", "pt3", "off3",
              "xz", "hv", "hs",
              "mm1", "mm2", "mm0", "mm3a", "mm3b", "ev1", "ev2", "ev0", "ev3a", "ev3b",
              "st1", "st2", "st0", "st3a", "st3b"]
SEMAPHORES += ["%s%d" % (n, k) for n in ("wi", "we", "wv", "wd", "qw", "xc", "qx", "xl", "xf", "xe") for k in range(NR)]
SEMAPHORES += ["%s%d" % (n, k) for n in ("lst", "arr") for k in range(1, NR)]
SEMAPHORES += ["ga%d%d" % (k, t) for k in range(NR) if k != WIN for t in range(4)]

COPY = ActivationFunctionType.Copy
AND, SHR, ADD, MULT = AluOpType.bitwise_and, AluOpType.arith_shift_right, AluOpType.add, AluOpType.mult


def rank_program(g, core, T, topo):
    me = T.rank_of(core)
    if me is None:
        return
    S = T.sem
    cores = T.cores
    v, a, te, sy = g.vector, g.scalar, g.tensor, g.sync

    def direct(k):
        return sum(1 for r in range(NR)
                   if topo.same_plane(topo.chip(cores[r]), topo.chip(cores[(r + k) % NR])))
    steps = [0] + sorted(range(1, NR), key=direct)
    to = [(me + steps[k]) % NR for k in range(NR)]
    frm = [(me - steps[k]) % NR for k in range(NR)]
    worder = [1, 0, 2, 3]

    def dst(r):
        rid, pid, _ = topo.addr(cores[r])
        return rid, pid

    def bits(engs):
        return sum(1 << e for e in engs)

    off_chip = topo.engines(core, cores[frm[1]])
    la, lb, lc = off_chip[0:4], off_chip[4:6], off_chip[6:8]

    sy.dma_start(T.pk[:], T.pick[:]).then_inc(S.pk, 16)
    sy.dma_start(T.wb[:], T.w[:]).then_inc(S.wl, 16)
    for n in range(16):
        z, q = n // 4, n % 4
        if n == 2:
            sy.wait_ge(S.ls1, len(la))
        if q == 0 and z >= 2:
            sy.wait_ge(S["xl%d" % (z - 2)], 64)
        sy.dma_start(T.xb[32 * q:32 * q + 32, 2048 * z:2048 * z + 2048],
                     T.x[512 * z:512 * z + 512, 128 * q:128 * q + 128]).then_inc(S["xl%d" % z], 16)

    v.memset(T.ones[:], 1.0).then_inc(S.id0, 1)
    v.wait_ge(S.pk, 16)
    v.tensor_scalar(T.plo[:], T.pk[:], 15, None, AND).then_inc(S.pa, 1)
    v.tensor_scalar(T.phi[:], T.pk[:], 4, None, SHR).then_inc(S.pb, 1)
    v.wait_ge(S.pa, 1)
    v.tensor_scalar(T.pls[:], T.plo[:], 128, None, MULT).then_inc(S.pc, 1)
    v.wait_ge(S.pb, 1)
    v.wait_ge(S.pc, 1)
    for q in range(8):
        v.tensor_tensor(T.pf[:, 16 * q:16 * q + 16], T.pls[:], T.phi[:], ADD).then_inc(S.pf, 1)
    v.wait_ge(S.wl, 16)
    for h in range(2):
        v.tensor_copy(T.wf[:, 1024 * h:1024 * h + 1024], T.wb[:, 1024 * h:1024 * h + 1024]).then_inc(S["wc%d" % h], 1)
    v.wait_ge(S.pt, 1)
    v.tensor_copy(T.offs[:], T.ps_p[:, 0:128]).then_inc(S.off, 1)
    li = T["li%d" % WIN]
    v.wait_ge(S["lst%d" % WIN], len(lc))
    v.tensor_scalar(T.lu[:], li[:], 5, 48, SHR, AND).then_inc(S.la, 1)
    v.tensor_scalar(T.lb[:], li[:], 15, None, AND).then_inc(S.la, 1)
    v.tensor_scalar(T.lc[:], li[:], 4, 31, SHR, AND).then_inc(S.la, 1)
    v.wait_ge(S.la, 3)
    v.tensor_tensor(T.lv[:], T.lu[:], T.lb[:], ADD).then_inc(S.lv, 1)
    v.wait_ge(S.lv, 1)
    v.tensor_scalar(T.lw[:], T.lv[:], 128, None, MULT).then_inc(S.lw, 1)
    v.wait_ge(S.lw, 1)
    v.tensor_tensor(T.lp[:], T.lw[:], T.lc[:], ADD).then_inc(S.lp, 1)
    v.wait_ge(S.lp, 1)
    for m in range(4):
        v.tensor_scalar(T.pf3[:, 4 * m:4 * m + 4], T.lp[:], 32 * m, None, ADD).then_inc(S.lm, 1)
    v.wait_ge(S.lm, 4)
    v.tensor_copy(T.pf3[:, 16:32], T.pf3[:, 0:16]).then_inc(S.ld1, 1)
    v.wait_ge(S.ld1, 1)
    v.tensor_copy(T.pf3[:, 32:64], T.pf3[:, 0:32]).then_inc(S.ld2, 1)
    v.wait_ge(S.ld2, 1)
    v.tensor_copy(T.pf3[:, 64:128], T.pf3[:, 0:64]).then_inc(S.ld3, 1)

    for b in range(4):
        a.wait_ge(S["wi%d" % b], 4)
        o = 512 * (b % 2)
        a.activation(T.wtr[:, 512 * b:512 * b + 512], T.ps_w[:, o:o + 512], COPY).then_inc(S["we%d" % b], 1)
    a.wait_ge(S.off, 1)
    for b in range(4):
        a.wait_ge(S["we%d" % b], 1)
    a.activation(T.wg[:], T.wtr[:].indirect(T.offs[:, 0:128]), COPY).then_inc(S.gs, 1)

    te.wait_ge(S.id1, 1)
    te.wait_ge(S.pf, 8)
    te.transpose(T.ps_p[:, 0:128], T.pf[:], T.ident[:]).then_inc(S.pt, 1)
    for b in range(4):
        if b % 2 == 0:
            te.wait_ge(S["wc%d" % (b // 2)], 1)
        if b >= 2:
            te.wait_ge(S["we%d" % (b - 2)], 1)
        for i in range(4):
            c = 4 * b + i
            o = 512 * (b % 2) + 128 * i
            te.transpose(T.ps_w[:, o:o + 128], T.wf[:, 128 * c:128 * c + 128], T.ident[:]).then_inc(S["wi%d" % b], 1)
    te.wait_ge(S.off, 1)
    te.wait_ge(S.ld3, 1)
    te.transpose(T.ps_p[:, 128:256], T.pf3[:], T.ident[:]).then_inc(S.pt3, 1)

    def wturn(n):
        k, o = worder[n], 512 * (n % 2)
        if n >= 2:
            te.wait_ge(S["wd%d" % worder[n - 2]], 1)
        for t in range(4):
            te.transpose(T.ps_w[:, o + t:o + 512:4], T.wg[:, 4 * frm[k] + t:2048:16], T.ident[:]).then_inc(S["wv%d" % k], 1)

    def wevac(n):
        k, o = worder[n], 512 * (n % 2)
        a.wait_ge(S["wv%d" % k], 4)
        a.activation(T["wt%d" % k][:], T.ps_w[:, o:o + 512], COPY).then_inc(S["wd%d" % k], 1)

    te.wait_ge(S.gs, 1)
    wturn(0)
    wturn(1)
    te.wait_ge(S.hv, 1)
    te.wait_ge(S.hs, 1)
    for m in range(4):
        if m >= 2:
            te.wait_ge(S["xe%d" % (m - 2)], 1)
        o = 512 * (m % 2)
        for t in range(4):
            te.transpose(T.ps_x[:, o + t:o + 512:4], T.xg[:, 4 * m + t:2048:16], T.ident[:]).then_inc(S["xf%d" % m], 1)
    wturn(2)
    wturn(3)

    a.wait_ge(S.off3, 1)
    a.wait_ge(S.xz, 4)
    a.activation(T.xg[:, 1024:2048], T.xv[:].indirect(T.offs3[:, 64:128]), COPY).then_inc(S.hs, 1)
    wevac(0)
    wevac(1)
    for m in range(4):
        a.wait_ge(S["xf%d" % m], 4)
        o = 512 * (m % 2)
        a.activation(T.x3[:, :, 128 * m:128 * m + 128], T.ps_x[:, o:o + 512], COPY).then_inc(S["xe%d" % m], 1)
    wevac(2)
    wevac(3)

    def xcopy(k, t):
        v.wait_ge(S["ga%d%d" % (k, t)], 16)
        v.tensor_copy(T["xt%d" % k][:, t:2048:4], T["xs%d" % k][:, 512 * t:512 * t + 512]).then_inc(S["xc%d" % k], 1)

    def xquant(k):
        v.wait_ge(S["xc%d" % k], 4)
        v.quantize_mx(T["xq%d" % k][:], T["xp%d" % k][:], T["xt%d" % k][:]).then_inc(S["qx%d" % k], 1)

    def wquant(n):
        k = worder[n]
        v.wait_ge(S["wd%d" % k], 1)
        v.quantize_mx(T["wq%d" % k][:], T["wp%d" % k][:], T["wt%d" % k][:]).then_inc(S["qw%d" % k], 1)

    def xturn(z):
        v.wait_ge(S["xl%d" % z], 64)
        v.transpose(T.xv[:, 2048 * z:2048 * z + 2048], T.xb[:, 2048 * z:2048 * z + 2048]).then_inc(S.xz, 1)

    xturn(0)
    v.wait_ge(S.pt3, 1)
    v.tensor_copy(T.offs3[:], T.ps_p[:, 128:256]).then_inc(S.off3, 1)
    xturn(1)
    xcopy(1, 0)
    xcopy(1, 1)
    xcopy(1, 2)
    xturn(2)
    xcopy(1, 3)
    xquant(1)
    xturn(3)
    v.wait_ge(S.off3, 1)
    v.wait_ge(S.xz, 4)
    v.tensor_copy(T.xg[:, 0:1024], T.xv[:].indirect(T.offs3[:, 0:64])).then_inc(S.hv, 1)
    for t in range(4):
        xcopy(2, t)
    xquant(2)
    for m in range(4):
        v.wait_ge(S["xe%d" % m], 1)
    for q in range(4):
        v.quantize_mx(T["xq%d" % WIN][:, 128 * q:128 * q + 128], T["xp%d" % WIN][:, 128 * q:128 * q + 128],
                      T.x3[:, q, :]).then_inc(S["qx%d" % WIN], 1)
    wquant(0)
    wquant(1)
    for t in range(4):
        xcopy(0, t)
    xquant(0)
    wquant(2)
    wquant(3)

    g.wait_ge(S.id0, 1)
    g.affine_select(T.ident[:], T.ones[:], [[-1, 128]], AluOpType.is_equal, 0.0, 0, 1).then_inc(S.id1, 1)

    def listmove(k, engs):
        s = frm[k]
        rid, pid = dst(s)
        return RemoteDMATransfer(dst_ids=[DstId(rid=rid, pnc=pid)], dma_engine_mask=bits(engs),
                                 remote_sem=S["lst%d" % k],
                                 srcs=[T.pk[:, 4 * s:4 * s + 4]], dsts=[T["li%d" % k][:]])

    def gather(k, t):
        idx = T["li%d" % k][:, t:t + 1] if k else T.pk[:, 4 * me + t:4 * me + t + 1]
        g.indirect_dma_start(T["xs%d" % k][:, 512 * t:512 * t + 512], None, T.x[:],
                             IndirectOffsetOnAxis(ap=idx, axis=0), bounds_check=ROWS - 1).then_inc(S["ga%d%d" % (k, t)], 16)

    def send_fused(k):
        e = topo.engines(core, cores[to[k]])
        rid, pid = dst(to[k])
        parts = [e[0:2], e[2:4], e[4:6], e[6:7], e[7:8]]
        tr = []
        for i, p in enumerate(parts):
            if i < 4:
                src = T["xq%d" % k][:, 128 * i:128 * i + 128].bitcast(dt.uint8)
                d = T["rq%d" % k][:, 128 * i:128 * i + 128].bitcast(dt.uint8)
            else:
                src, d = T["xp%d" % k][:], T["rp%d" % k][:]
            tr.append(RemoteDMATransfer(dst_ids=[DstId(rid=rid, pnc=pid)], dma_engine_mask=bits(p),
                                        remote_sem=S["arr%d" % k], srcs=[src], dsts=[d]))
        g.remote_dma_fused(tr, local_sem=S.csent)
        return sum(len(p) for p in parts)

    def send_two(k):
        e = topo.engines(core, cores[to[k]])
        rid, pid = dst(to[k])
        g.remote_dma(T["rq%d" % k][:].bitcast(dt.uint8), T["xq%d" % k][:].bitcast(dt.uint8),
                     S["arr%d" % k], S.csent, pid, rid, bits(e))
        g.remote_dma(T["rp%d" % k][:], T["xp%d" % k][:], S["arr%d" % k], S.csent, pid, rid, bits(e))
        return 2 * len(e)

    g.wait_ge(S.pk, 16)
    g.remote_dma_fused([listmove(1, la)], local_sem=S.ls1)
    gather(0, 0)
    g.remote_dma_fused([listmove(2, lb), listmove(3, lc)], local_sem=S.lsent)
    gather(0, 1)
    g.wait_ge(S.lst1, len(la))
    for t in range(4):
        gather(1, t)
    g.wait_ge(S.lst2, len(lb))
    for t in range(3):
        gather(2, t)
    g.wait_ge(S.qx1, 1)
    n1 = send_fused(1)
    gather(2, 3)
    gather(0, 2)
    gather(0, 3)
    g.wait_ge(S.qx2, 1)
    n2 = send_two(2)
    g.wait_ge(S["qx%d" % WIN], 4)
    n3 = send_two(WIN)
    g.wait_ge(S.lsent, len(lb) + len(lc))
    g.wait_ge(S.csent, n1 + n2 + n3)

    bank = {1: 0, 0: 512, 2: 1024}
    narr = {1: n1, 2: n2}
    for k in worder[:3]:
        o = bank[k]
        te.wait_ge(S["qw%d" % k], 1)
        if k:
            te.wait_ge(S["arr%d" % k], narr[k])
            xq, xp = T["rq%d" % k], T["rp%d" % k]
        else:
            te.wait_ge(S.qx0, 1)
            xq, xp = T.xq0, T.xp0
        te.matmul_mx(T.ps_y[:, o:o + 512], T["wq%d" % k][:], T["wp%d" % k][:], xq[:], xp[:], True, True).then_inc(S["mm%d" % k], 1)
    te.wait_ge(S.qw3, 1)
    te.wait_ge(S.ev1, 1)
    te.wait_ge(S.ev0, 1)
    te.wait_ge(S.arr3, n3)
    te.matmul_mx(T.ps_y[:, 0:256], T.wq3[:], T.wp3[:], T.rq3[:, 0:256], T.rp3[:, 0:256], True, True).then_inc(S.mm3a, 1)
    te.matmul_mx(T.ps_y[:, 512:768], T.wq3[:], T.wp3[:], T.rq3[:, 256:512], T.rp3[:, 256:512], True, True).then_inc(S.mm3b, 1)

    def ycols(k, lo=0, hi=XC):
        b = XC * frm[k]
        return slice(b + lo, b + hi)

    for k in worder[:3]:
        o = bank[k]
        a.wait_ge(S["mm%d" % k], 1)
        a.activation(T.ys[:, ycols(k)], T.ps_y[:, o:o + 512], COPY).then_inc(S["ev%d" % k], 1)
        sy.wait_ge(S["ev%d" % k], 1)
        sy.dma_start(T.y[:, ycols(k)], T.ys[:, ycols(k)]).then_inc(S["st%d" % k], 16)
    v.wait_ge(S.mm3a, 1)
    v.tensor_copy(T.ys[:, ycols(3, 0, 256)], T.ps_y[:, 0:256]).then_inc(S.ev3a, 1)
    sy.wait_ge(S.ev3a, 1)
    sy.dma_start(T.y[:, ycols(3, 0, 256)], T.ys[:, ycols(3, 0, 256)]).then_inc(S.st3a, 16)
    a.wait_ge(S.mm3b, 1)
    a.activation(T.ys[:, ycols(3, 256, 512)], T.ps_y[:, 512:768], COPY).then_inc(S.ev3b, 1)
    a.wait_ge(S.ev3b, 1)
    a.dma_start(T.y[:, ycols(3, 256, 512)], T.ys[:, ycols(3, 256, 512)]).then_inc(S.st3b, 16)
    for n in ("st1", "st2", "st0", "st3a"):
        sy.wait_ge(S[n], 16)
    a.wait_ge(S.st3b, 16)
